import numpy as np
import ml_dtypes


def mxq(x, axis, fmt="e4m3"):
    dtype, down = {"e4m3": (ml_dtypes.float8_e4m3fn, 7), "e5m2": (ml_dtypes.float8_e5m2, 14)}[fmt]
    v = np.moveaxis(np.asarray(x, np.float32).astype(ml_dtypes.bfloat16).astype(np.float64), axis, -1)
    blocks = v.reshape(v.shape[:-1] + (-1, 32))
    amax = np.abs(blocks).max(-1, keepdims=True)
    byte = np.maximum(np.where(amax > 0, np.frexp(amax)[1] - 1 + 127, 0) - down, 1)
    scale = np.exp2(byte - 127.0)
    codes = (blocks / scale).astype(np.float32).astype(dtype).astype(np.float64)
    return np.moveaxis((codes * scale).reshape(v.shape), -1, axis)


WIDE = False


def mx_kscale(k):
    if not WIDE:
        return np.ones(k)
    levels = np.array([10, -10, 5, -5, 0])
    if k % 512:
        return np.exp2(np.random.permutation(np.resize(levels, k // 32))).repeat(32)
    a = np.empty((k // 512, 16))
    for p in range(k // 512):
        a[p, :8] = np.random.permutation(np.resize(levels, 8))
        for g in range(8):
            far = levels[np.abs(levels - a[p, g]) >= 10]
            a[p, g + 8] = far[np.random.randint(len(far))]
    return np.exp2(a.ravel()).repeat(32)


def f64(x):
    return np.asarray(x).astype(np.float64)


def striped(idx):
    return np.tile(idx.reshape(-1, 16).T, (8, 1)).astype(np.uint16)


def unstriped(offs):
    return offs[:16].T.reshape(-1).astype(np.int64)


E2M1 = np.array([0.0, 0.5, 1.0, 1.5, 2.0, 3.0, 4.0, 6.0, -0.0, -0.5, -1.0, -1.5, -2.0, -3.0, -4.0, -6.0])


def pack_weight(w, fmt):
    k, n = w.shape
    w = f64(np.asarray(w, np.float32).astype(ml_dtypes.bfloat16)).reshape(k // 32, 32, n)
    amax = np.abs(w).max(1)
    if fmt == "e4m3":
        byte = np.frexp(amax)[1] - 1 + 127 - 7
    else:
        mant, ex = np.frexp(amax / 6.0)
        byte = np.where(mant > 0.5, ex, ex - 1) + 127
    byte = np.clip(np.where(amax > 0, byte, 1), 1, 254)
    scaled = (w * np.exp2(127.0 - byte)[:, None, :]).reshape(k, n).astype(np.float32)
    by_word = np.ascontiguousarray(scaled.reshape(k // 512, 128, 4, n).transpose(0, 1, 3, 2))
    if fmt == "e4m3":
        words = by_word.astype(ml_dtypes.float8_e4m3fn).view(np.uint8)
    else:
        c = by_word.astype(ml_dtypes.float4_e2m1fn).view(np.uint8) & 0xF
        words = (c[..., 0::2] | (c[..., 1::2] << 4)).reshape(k // 512, 128, 2 * n)
    return np.ascontiguousarray(words), np.ascontiguousarray(byte.astype(np.uint8).reshape(k // 512, 16, n))


def unpack_weight(words, scales, fmt):
    g, _, n = scales.shape
    words = np.ascontiguousarray(words).reshape(g, 128, n, -1)
    if fmt == "e4m3":
        vals = words.view(ml_dtypes.float8_e4m3fn).astype(np.float64)
    else:
        nib = np.empty((g, 128, n, 4), np.uint8)
        nib[..., 0::2] = words & 0xF
        nib[..., 1::2] = words >> 4
        vals = E2M1[nib]
    vals = vals * np.repeat(np.exp2(scales.astype(np.float64) - 127.0), 8, axis=1)[..., None]
    return vals.transpose(0, 1, 3, 2).reshape(g * 512, n)


K, T, E, C, N = 1536, 512, 4, 128, 384


def by_expert(wq, xq):
    return np.concatenate([wq[e].T @ xq[:, e * C:(e + 1) * C] for e in range(E)], axis=1)


def setup_inputs():
    n = np.random.standard_normal
    s = mx_kscale(K)[:, None]
    w = [pack_weight(m, "e2m1") for m in n((E, K, N)) / np.sqrt(K) / s[None]]
    return {
        "xT": (n((K, T)) * s).astype(np.float32),
        "w_words": np.stack([m[0] for m in w]),
        "w_scales": np.stack([m[1] for m in w]),
        "b": (0.3 * n((N, E))).astype(np.float32),
        "gate": np.tile(np.random.uniform(0.2, 1.0, E * C), (N, 1)).astype(np.float32),
        "offs": striped(np.random.permutation(T)[:E * C]),
    }


def reference(xT, w_words, w_scales, b, gate, offs):
    idx = unstriped(offs)
    w = np.stack([unpack_weight(w_words[e], w_scales[e], "e2m1") for e in range(E)])
    xq = mxq(f64(xT)[:, idx], 0, "e4m3")
    y = by_expert(w, xq)
    y = y + np.repeat(f64(b), C, axis=1)
    out = np.zeros((N, T))
    out[:, idx] = f64(gate) * y
    return out

@@ -1,0 +1,176 @@
+from contextlib import ExitStack
+
+import concourse.mybir as mybir
+
+K, T, E, C, N = 1536, 512, 4, 128, 384
+FLOPS = 2 * K * E * C * N
+
+F32 = mybir.dt.float32
+BF16 = mybir.dt.bfloat16
+I32 = mybir.dt.int32
+U32 = mybir.dt.uint32
+U16 = mybir.dt.uint16
+U8 = mybir.dt.uint8
+FP8X4 = mybir.dt.float8_e4m3fn_x4
+FP4X4 = mybir.dt.float4_e2m1fn_x4
+MULT = mybir.AluOpType.mult
+COPY = mybir.ActivationFunctionType.Copy
+IDENTITY = mybir.ActivationFunctionType.Identity
+
+P = 128
+PACK = 4
+PASSES = K // (P * PACK)
+NT = N // P
+HALF = T // 2
+WINDOW = 704
+VCOLS = 160
+
+
+def tile_moe_pln_lin_bias_kernel(tc, xT, w_words, w_scales, b, gate, offs, out):
+    nc = tc.nc
+    with ExitStack() as ctx:
+        lists = ctx.enter_context(tc.tile_pool(name="lists", bufs=1))
+        keep = ctx.enter_context(tc.tile_pool(name="keep", bufs=1))
+        psum = ctx.enter_context(tc.psum_pool(name="psum", bufs=8))
+
+        offsets = lists.tile([P, T // 16], U16, name="offsets")
+
+        raw = [[keep.tile([P, PACK, HALF], F32, name=f"raw{a}{h}") for h in range(2)] for a in range(PASSES)]
+        grouped = [[keep.tile([P, HALF * PACK], BF16, name=f"grouped{a}{h}", align_bytes=64) for h in range(2)] for a in range(PASSES)]
+        tok_words = [keep.tile([P, WINDOW], I32, name=f"tok_words{a}", align_bytes=64) for a in range(PASSES)]
+        tok_scales = [keep.tile([P, WINDOW], U8, name=f"tok_scales{a}", align_bytes=64) for a in range(PASSES)]
+        slot_words = [keep.tile([P, E * C], U32, name=f"slot_words{a}", align_bytes=64) for a in range(PASSES)]
+        slot_scales = [keep.tile([P, E * C], U8, name=f"slot_scales{a}", align_bytes=64) for a in range(PASSES)]
+        words = keep.tile([P, E * PASSES, 2 * N], U8, name="words", align_bytes=64)
+        scales = keep.tile([P, E * PASSES, N], U8, name="scales", align_bytes=64)
+        bias = keep.tile([P, NT, E], F32, name="bias")
+        gates = [keep.tile([P, E * C], F32, name=f"gates{t}") for t in range(NT)]
+        y = [keep.tile([P, E * C], F32, name=f"y{t}") for t in range(NT)]
+        result = [keep.tile([P, WINDOW], F32, name=f"result{t}") for t in range(NT)]
+        warm = keep.tile([P, 2], F32, name="warm")
+
+        def load_x(a, h):
+            rows = xT[a * P * PACK : (a + 1) * P * PACK, h * HALF : (h + 1) * HALF]
+            nc.sync.dma_start(out=raw[a][h][:], in_=rows.rearrange("(p j) c -> p j c", j=PACK))
+
+        def load_words(e):
+            nc.sync.dma_start(
+                out=words[:, e * PASSES : (e + 2) * PASSES, :].bitcast(I32),
+                in_=w_words[e : e + 2].bitcast(I32).rearrange("e a p n -> p (e a) n"),
+            )
+
+        def load_gate(t):
+            nc.sync.dma_start(out=gates[t][:], in_=gate[t * P : (t + 1) * P, :])
+
+        load_x(0, 0)
+        load_x(0, 1)
+        nc.sync.dma_start(offsets[:], offs)
+        nc.scalar.dma_start(out=bias[:], in_=b.rearrange("(t p) e -> p t e", p=P))
+
+        nc.vector.memset(warm[:], 0.0)
+        nc.scalar.activation(warm[:, 1:2], warm[:, 0:1], IDENTITY)
+        for a in range(PASSES):
+            nc.gpsimd.memset(tok_scales[a][:], 0)
+        nc.vector.memset(scales[:].bitcast(I32), 0)
+        for a in range(PASSES):
+            nc.vector.memset(tok_words[a][:, T:], 0)
+
+        load_x(1, 0)
+        load_x(1, 1)
+        load_x(2, 0)
+        load_x(2, 1)
+        w_scale_rows = w_scales.bitcast(I32).rearrange("e a (q r) n -> r q (e a) n", r=4)
+        for r in range(4):
+            nc.sync.dma_start(out=scales[r:P:32, :, :].bitcast(I32), in_=w_scale_rows[r])
+        load_words(0)
+        load_gate(0)
+        load_words(2)
+        load_gate(1)
+        load_gate(2)
+
+        def group(engine_copy, a, h, c0, c1):
+            dst = grouped[a][h][:].rearrange("p (c j) -> p c j", j=PACK)[:, c0:c1, :]
+            src = raw[a][h][:].rearrange("p j c -> p c j")[:, c0:c1, :]
+            engine_copy(dst, src)
+
+        def vector_group(dst, src):
+            nc.vector.tensor_copy(out=dst, in_=src)
+
+        def scalar_group(dst, src):
+            nc.scalar.activation(dst, src, COPY)
+
+        def quantise(a, h):
+            cols = slice(h * HALF, (h + 1) * HALF)
+            nc.vector.quantize_mx(out=tok_words[a][:, cols].bitcast(FP8X4), scales=tok_scales[a][:, cols], in_=grouped[a][h][:])
+
+        def gather_words(a, s0, s1):
+            nc.vector.tensor_copy(slot_words[a][:, s0:s1], tok_words[a][:].bitcast(U32).indirect(offsets[:, s0 // 16 : s1 // 16]))
+
+        def gather_scales(a, s0, s1):
+            nc.vector.tensor_copy(slot_scales[a][:, s0:s1], tok_scales[a][:].indirect(offsets[:, s0 // 16 : s1 // 16]))
+
+        banks = {}
+
+        def multiply(a, t, e):
+            if a == 0:
+                banks[t, e] = psum.tile([P, C], F32, name="bank")
+            ea = e * PASSES + a
+            nc.tensor.matmul_mx(
+                out=banks[t, e][:],
+                lhsT=words[:, ea, 2 * P * t : 2 * P * (t + 1)].bitcast(FP4X4),
+                lhsT_scale=scales[:, ea, P * t : P * (t + 1)],
+                rhs=slot_words[a][:, e * C : (e + 1) * C].bitcast(FP8X4),
+                rhs_scale=slot_scales[a][:, e * C : (e + 1) * C],
+                start=(a == 0),
+                stop=(a == PASSES - 1),
+            )
+
+        def leave_bank(t, e):
+            nc.scalar.activation(y[t][:, e * C : (e + 1) * C], banks[t, e][:], IDENTITY, bias=bias[:, t, e : e + 1])
+
+        def scatter(t, s0, s1):
+            nc.vector.tensor_tensor(result[t][:].indirect(offsets[:, s0 // 16 : s1 // 16]), y[t][:, s0:s1], gates[t][:, s0:s1], MULT)
+
+        def store(t):
+            nc.sync.dma_start(out=out[t * P : (t + 1) * P, :], in_=result[t][:, :T])
+
+        S = E * C
+        for h in range(2):
+            group(vector_group, 0, h, 0, VCOLS)
+            group(scalar_group, 0, h, VCOLS, HALF)
+            quantise(0, h)
+        group(scalar_group, 1, 0, 0, HALF)
+        group(scalar_group, 1, 1, 0, HALF)
+        gather_words(0, 0, S)
+        quantise(1, 0)
+        gather_scales(0, 0, S)
+        quantise(1, 1)
+        group(scalar_group, 2, 0, 0, HALF)
+        group(scalar_group, 2, 1, 0, HALF)
+        for t in range(2):
+            for e in range(E):
+                multiply(0, t, e)
+        gather_words(1, 0, S)
+        quantise(2, 0)
+        gather_scales(1, 0, S)
+        quantise(2, 1)
+        for t in range(2):
+            for e in range(E):
+                multiply(1, t, e)
+        for s0 in (0, HALF):
+            gather_words(2, s0, s0 + HALF)
+            gather_scales(2, s0, s0 + HALF)
+            for t in range(2):
+                for e in (s0 // C, s0 // C + 1):
+                    multiply(2, t, e)
+                    leave_bank(t, e)
+        for e in range(E):
+            for a in range(PASSES):
+                multiply(a, 2, e)
+            leave_bank(2, e)
+        scatter(0, 0, HALF)
+        scatter(0, HALF, S)
+        store(0)
+        for t in range(1, NT):
+            scatter(t, 0, S)
+            store(t)

@@ -23,7 +23,7 @@ PASSES = K // (P * PACK)
 NT = N // P
 HALF = T // 2
 WINDOW = 704
-VCOLS = 160
+VCOLS = 128
 
 
 def tile_moe_pln_lin_bias_kernel(tc, xT, w_words, w_scales, b, gate, offs, out):
@@ -35,7 +35,7 @@ def tile_moe_pln_lin_bias_kernel(tc, xT, w_words, w_scales, b, gate, offs, out):
 
         offsets = lists.tile([P, T // 16], U16, name="offsets")
 
-        raw = [[keep.tile([P, PACK, HALF], F32, name=f"raw{a}{h}") for h in range(2)] for a in range(PASSES)]
+        raw = [keep.tile([P, PACK, T], F32, name=f"raw{a}") for a in range(PASSES)]
         grouped = [[keep.tile([P, HALF * PACK], BF16, name=f"grouped{a}{h}", align_bytes=64) for h in range(2)] for a in range(PASSES)]
         tok_words = [keep.tile([P, WINDOW], I32, name=f"tok_words{a}", align_bytes=64) for a in range(PASSES)]
         tok_scales = [keep.tile([P, WINDOW], U8, name=f"tok_scales{a}", align_bytes=64) for a in range(PASSES)]
@@ -49,9 +49,9 @@ def tile_moe_pln_lin_bias_kernel(tc, xT, w_words, w_scales, b, gate, offs, out):
         result = [keep.tile([P, WINDOW], F32, name=f"result{t}") for t in range(NT)]
         warm = keep.tile([P, 2], F32, name="warm")
 
-        def load_x(a, h):
-            rows = xT[a * P * PACK : (a + 1) * P * PACK, h * HALF : (h + 1) * HALF]
-            nc.sync.dma_start(out=raw[a][h][:], in_=rows.rearrange("(p j) c -> p j c", j=PACK))
+        def load_x(a):
+            rows = xT[a * P * PACK : (a + 1) * P * PACK, :]
+            nc.sync.dma_start(out=raw[a][:], in_=rows.rearrange("(p j) c -> p j c", j=PACK))
 
         def load_words(e):
             nc.sync.dma_start(
@@ -62,8 +62,7 @@ def tile_moe_pln_lin_bias_kernel(tc, xT, w_words, w_scales, b, gate, offs, out):
         def load_gate(t):
             nc.sync.dma_start(out=gates[t][:], in_=gate[t * P : (t + 1) * P, :])
 
-        load_x(0, 0)
-        load_x(0, 1)
+        load_x(0)
         nc.sync.dma_start(offsets[:], offs)
         nc.scalar.dma_start(out=bias[:], in_=b.rearrange("(t p) e -> p t e", p=P))
 
@@ -75,22 +74,20 @@ def tile_moe_pln_lin_bias_kernel(tc, xT, w_words, w_scales, b, gate, offs, out):
         for a in range(PASSES):
             nc.vector.memset(tok_words[a][:, T:], 0)
 
-        load_x(1, 0)
-        load_x(1, 1)
-        load_x(2, 0)
-        load_x(2, 1)
+        load_x(1)
+        load_x(2)
+        load_words(0)
         w_scale_rows = w_scales.bitcast(I32).rearrange("e a (q r) n -> r q (e a) n", r=4)
         for r in range(4):
             nc.sync.dma_start(out=scales[r:P:32, :, :].bitcast(I32), in_=w_scale_rows[r])
-        load_words(0)
         load_gate(0)
         load_words(2)
         load_gate(1)
         load_gate(2)
 
         def group(engine_copy, a, h, c0, c1):
-            dst = grouped[a][h][:].rearrange("p (c j) -> p c j", j=PACK)[:, c0:c1, :]
-            src = raw[a][h][:].rearrange("p j c -> p c j")[:, c0:c1, :]
+            dst = grouped[a][h][:, c0 * PACK : c1 * PACK].rearrange("p (c i j) -> p c j i", i=4, j=PACK)
+            src = raw[a][:, :, h * HALF + c0 : h * HALF + c1].rearrange("p j (c i) -> p c j i", i=4)
             engine_copy(dst, src)
 
         def vector_group(dst, src):
@@ -138,6 +135,7 @@ def tile_moe_pln_lin_bias_kernel(tc, xT, w_words, w_scales, b, gate, offs, out):
         for h in range(2):
             group(vector_group, 0, h, 0, VCOLS)
             group(scalar_group, 0, h, VCOLS, HALF)
+        for h in range(2):
             quantise(0, h)
         group(scalar_group, 1, 0, 0, HALF)
         group(scalar_group, 1, 1, 0, HALF)

@@ -24,6 +24,7 @@ NT = N // P
 HALF = T // 2
 WINDOW = 704
 VCOLS = 128
+V1 = 96
 
 
 def tile_moe_pln_lin_bias_kernel(tc, xT, w_words, w_scales, b, gate, offs, out):
@@ -31,7 +32,7 @@ def tile_moe_pln_lin_bias_kernel(tc, xT, w_words, w_scales, b, gate, offs, out):
     with ExitStack() as ctx:
         lists = ctx.enter_context(tc.tile_pool(name="lists", bufs=1))
         keep = ctx.enter_context(tc.tile_pool(name="keep", bufs=1))
-        psum = ctx.enter_context(tc.psum_pool(name="psum", bufs=8))
+        psum = ctx.enter_context(tc.psum_pool(name="psum", bufs=4))
 
         offsets = lists.tile([P, T // 16], U16, name="offsets")
 
@@ -62,9 +63,10 @@ def tile_moe_pln_lin_bias_kernel(tc, xT, w_words, w_scales, b, gate, offs, out):
         def load_gate(t):
             nc.sync.dma_start(out=gates[t][:], in_=gate[t * P : (t + 1) * P, :])
 
-        load_x(0)
+        for u in range(2):
+            rows = xT[: P * PACK, :].rearrange("(p j) c -> p j c", j=PACK)
+            nc.sync.dma_start(out=raw[0][:, 2 * u : 2 * u + 2, :], in_=rows[:, 2 * u : 2 * u + 2, :])
         nc.sync.dma_start(offsets[:], offs)
-        nc.scalar.dma_start(out=bias[:], in_=b.rearrange("(t p) e -> p t e", p=P))
 
         nc.vector.memset(warm[:], 0.0)
         nc.scalar.activation(warm[:, 1:2], warm[:, 0:1], IDENTITY)
@@ -80,14 +82,20 @@ def tile_moe_pln_lin_bias_kernel(tc, xT, w_words, w_scales, b, gate, offs, out):
         w_scale_rows = w_scales.bitcast(I32).rearrange("e a (q r) n -> r q (e a) n", r=4)
         for r in range(4):
             nc.sync.dma_start(out=scales[r:P:32, :, :].bitcast(I32), in_=w_scale_rows[r])
+        nc.sync.dma_start(out=bias[:], in_=b.rearrange("(t p) e -> p t e", p=P))
         load_gate(0)
-        load_words(2)
         load_gate(1)
+        load_words(2)
         load_gate(2)
 
         def group(engine_copy, a, h, c0, c1):
             dst = grouped[a][h][:, c0 * PACK : c1 * PACK].rearrange("p (c i j) -> p c j i", i=4, j=PACK)
             src = raw[a][:, :, h * HALF + c0 : h * HALF + c1].rearrange("p j (c i) -> p c j i", i=4)
+            engine_copy(dst, src)
+
+        def group_pair(engine_copy, h, u, c0, c1):
+            dst = grouped[0][h][:, c0 * PACK : c1 * PACK].rearrange("p (c i j) -> p c j i", i=4, j=PACK)[:, :, 2 * u : 2 * u + 2, :]
+            src = raw[0][:, 2 * u : 2 * u + 2, h * HALF + c0 : h * HALF + c1].rearrange("p j (c i) -> p c j i", i=4)
             engine_copy(dst, src)
 
         def vector_group(dst, src):
@@ -132,43 +140,49 @@ def tile_moe_pln_lin_bias_kernel(tc, xT, w_words, w_scales, b, gate, offs, out):
             nc.sync.dma_start(out=out[t * P : (t + 1) * P, :], in_=result[t][:, :T])
 
         S = E * C
-        for h in range(2):
-            group(vector_group, 0, h, 0, VCOLS)
-            group(scalar_group, 0, h, VCOLS, HALF)
+        for u in range(2):
+            for h in range(2):
+                group_pair(vector_group, h, u, 0, VCOLS)
+                group_pair(scalar_group, h, u, VCOLS, HALF)
         for h in range(2):
             quantise(0, h)
         group(scalar_group, 1, 0, 0, HALF)
-        group(scalar_group, 1, 1, 0, HALF)
+        group(scalar_group, 1, 1, V1, HALF)
         gather_words(0, 0, S)
+        group(vector_group, 1, 1, 0, V1)
         quantise(1, 0)
-        gather_scales(0, 0, S)
+        gather_scales(0, 0, HALF)
         quantise(1, 1)
+        gather_scales(0, HALF, S)
         group(scalar_group, 2, 0, 0, HALF)
         group(scalar_group, 2, 1, 0, HALF)
-        for t in range(2):
-            for e in range(E):
-                multiply(0, t, e)
         gather_words(1, 0, S)
         quantise(2, 0)
-        gather_scales(1, 0, S)
+        gather_scales(1, 0, HALF)
         quantise(2, 1)
+        gather_scales(1, HALF, S)
+        for h in range(2):
+            gather_words(2, h * HALF, (h + 1) * HALF)
+            gather_scales(2, h * HALF, (h + 1) * HALF)
         for t in range(2):
-            for e in range(E):
-                multiply(1, t, e)
-        for s0 in (0, HALF):
-            gather_words(2, s0, s0 + HALF)
-            gather_scales(2, s0, s0 + HALF)
-            for t in range(2):
-                for e in (s0 // C, s0 // C + 1):
-                    multiply(2, t, e)
-                    leave_bank(t, e)
+            for e in range(2):
+                for a in range(2):
+                    multiply(a, t, e)
+        for t in range(2):
+            for e in range(2):
+                multiply(2, t, e)
+                leave_bank(t, e)
+            scatter(t, 0, HALF)
+        for t in range(2):
+            for e in range(2, E):
+                for a in range(PASSES):
+                    multiply(a, t, e)
+                leave_bank(t, e)
+            scatter(t, HALF, S)
+            store(t)
         for e in range(E):
             for a in range(PASSES):
                 multiply(a, 2, e)
             leave_bank(2, e)
-        scatter(0, 0, HALF)
-        scatter(0, HALF, S)
-        store(0)
-        for t in range(1, NT):
-            scatter(t, 0, S)
-            store(t)
+        scatter(2, 0, S)
+        store(2)

@@ -32,7 +32,7 @@ def tile_moe_pln_lin_bias_kernel(tc, xT, w_words, w_scales, b, gate, offs, out):
     with ExitStack() as ctx:
         lists = ctx.enter_context(tc.tile_pool(name="lists", bufs=1))
         keep = ctx.enter_context(tc.tile_pool(name="keep", bufs=1))
-        psum = ctx.enter_context(tc.psum_pool(name="psum", bufs=4))
+        psum = ctx.enter_context(tc.psum_pool(name="psum", bufs=3))
 
         offsets = lists.tile([P, T // 16], U16, name="offsets")
 
@@ -60,6 +60,11 @@ def tile_moe_pln_lin_bias_kernel(tc, xT, w_words, w_scales, b, gate, offs, out):
                 in_=w_words[e : e + 2].bitcast(I32).rearrange("e a p n -> p (e a) n"),
             )
 
+        def load_scales(e):
+            rows = w_scales[e : e + 2].bitcast(I32).rearrange("e a (q r) n -> r q (e a) n", r=4)
+            for r in range(4):
+                nc.sync.dma_start(out=scales[r:P:32, e * PASSES : (e + 2) * PASSES, :].bitcast(I32), in_=rows[r])
+
         def load_gate(t):
             nc.sync.dma_start(out=gates[t][:], in_=gate[t * P : (t + 1) * P, :])
 
@@ -78,13 +83,12 @@ def tile_moe_pln_lin_bias_kernel(tc, xT, w_words, w_scales, b, gate, offs, out):
 
         load_x(1)
         load_x(2)
+        load_scales(0)
         load_words(0)
-        w_scale_rows = w_scales.bitcast(I32).rearrange("e a (q r) n -> r q (e a) n", r=4)
-        for r in range(4):
-            nc.sync.dma_start(out=scales[r:P:32, :, :].bitcast(I32), in_=w_scale_rows[r])
         nc.sync.dma_start(out=bias[:], in_=b.rearrange("(t p) e -> p t e", p=P))
         load_gate(0)
         load_gate(1)
+        load_scales(2)
         load_words(2)
         load_gate(2)
 
@@ -166,11 +170,8 @@ def tile_moe_pln_lin_bias_kernel(tc, xT, w_words, w_scales, b, gate, offs, out):
             gather_scales(2, h * HALF, (h + 1) * HALF)
         for t in range(2):
             for e in range(2):
-                for a in range(2):
+                for a in range(PASSES):
                     multiply(a, t, e)
-        for t in range(2):
-            for e in range(2):
-                multiply(2, t, e)
                 leave_bank(t, e)
             scatter(t, 0, HALF)
         for t in range(2):

from contextlib import ExitStack

import concourse.mybir as mybir

K, T, E, C, N = 1536, 512, 4, 128, 384
FLOPS = 2 * K * E * C * N

F32 = mybir.dt.float32
BF16 = mybir.dt.bfloat16
I32 = mybir.dt.int32
U32 = mybir.dt.uint32
U16 = mybir.dt.uint16
U8 = mybir.dt.uint8
FP8X4 = mybir.dt.float8_e4m3fn_x4
FP4X4 = mybir.dt.float4_e2m1fn_x4
MULT = mybir.AluOpType.mult
COPY = mybir.ActivationFunctionType.Copy
IDENTITY = mybir.ActivationFunctionType.Identity

P = 128
PACK = 4
PASSES = K // (P * PACK)
NT = N // P
HALF = T // 2
WINDOW = 704
VCOLS = 128
V1 = 96


def tile_moe_pln_lin_bias_kernel(tc, xT, w_words, w_scales, b, gate, offs, out):
    nc = tc.nc
    with ExitStack() as ctx:
        lists = ctx.enter_context(tc.tile_pool(name="lists", bufs=1))
        keep = ctx.enter_context(tc.tile_pool(name="keep", bufs=1))
        psum = ctx.enter_context(tc.psum_pool(name="psum", bufs=3))

        offsets = lists.tile([P, T // 16], U16, name="offsets")

        raw = [keep.tile([P, PACK, T], F32, name=f"raw{a}") for a in range(PASSES)]
        grouped = [[keep.tile([P, HALF * PACK], BF16, name=f"grouped{a}{h}", align_bytes=64) for h in range(2)] for a in range(PASSES)]
        tok_words = [keep.tile([P, WINDOW], I32, name=f"tok_words{a}", align_bytes=64) for a in range(PASSES)]
        tok_scales = [keep.tile([P, WINDOW], U8, name=f"tok_scales{a}", align_bytes=64) for a in range(PASSES)]
        slot_words = [keep.tile([P, E * C], U32, name=f"slot_words{a}", align_bytes=64) for a in range(PASSES)]
        slot_scales = [keep.tile([P, E * C], U8, name=f"slot_scales{a}", align_bytes=64) for a in range(PASSES)]
        words = keep.tile([P, E * PASSES, 2 * N], U8, name="words", align_bytes=64)
        scales = keep.tile([P, E * PASSES, N], U8, name="scales", align_bytes=64)
        bias = keep.tile([P, NT, E], F32, name="bias")
        gates = [keep.tile([P, E * C], F32, name=f"gates{t}") for t in range(NT)]
        y = [keep.tile([P, E * C], F32, name=f"y{t}") for t in range(NT)]
        result = [keep.tile([P, WINDOW], F32, name=f"result{t}") for t in range(NT)]
        warm = keep.tile([P, 2], F32, name="warm")

        def load_x(a):
            rows = xT[a * P * PACK : (a + 1) * P * PACK, :]
            nc.sync.dma_start(out=raw[a][:], in_=rows.rearrange("(p j) c -> p j c", j=PACK))

        def load_words(e):
            nc.sync.dma_start(
                out=words[:, e * PASSES : (e + 2) * PASSES, :].bitcast(I32),
                in_=w_words[e : e + 2].bitcast(I32).rearrange("e a p n -> p (e a) n"),
            )

        def load_scales(e):
            rows = w_scales[e : e + 2].bitcast(I32).rearrange("e a (q r) n -> r q (e a) n", r=4)
            for r in range(4):
                nc.sync.dma_start(out=scales[r:P:32, e * PASSES : (e + 2) * PASSES, :].bitcast(I32), in_=rows[r])

        def load_gate(t):
            nc.sync.dma_start(out=gates[t][:], in_=gate[t * P : (t + 1) * P, :])

        for u in range(2):
            rows = xT[: P * PACK, :].rearrange("(p j) c -> p j c", j=PACK)
            nc.sync.dma_start(out=raw[0][:, 2 * u : 2 * u + 2, :], in_=rows[:, 2 * u : 2 * u + 2, :])
        nc.sync.dma_start(offsets[:], offs)

        nc.vector.memset(warm[:], 0.0)
        nc.scalar.activation(warm[:, 1:2], warm[:, 0:1], IDENTITY)
        for a in range(PASSES):
            nc.gpsimd.memset(tok_scales[a][:], 0)
        nc.vector.memset(scales[:].bitcast(I32), 0)
        for a in range(PASSES):
            nc.vector.memset(tok_words[a][:, T:], 0)

        load_x(1)
        load_x(2)
        load_scales(0)
        load_words(0)
        nc.sync.dma_start(out=bias[:], in_=b.rearrange("(t p) e -> p t e", p=P))
        load_gate(0)
        load_gate(1)
        load_scales(2)
        load_words(2)
        load_gate(2)

        def group(engine_copy, a, h, c0, c1):
            dst = grouped[a][h][:, c0 * PACK : c1 * PACK].rearrange("p (c i j) -> p c j i", i=4, j=PACK)
            src = raw[a][:, :, h * HALF + c0 : h * HALF + c1].rearrange("p j (c i) -> p c j i", i=4)
            engine_copy(dst, src)

        def group_pair(engine_copy, h, u, c0, c1):
            dst = grouped[0][h][:, c0 * PACK : c1 * PACK].rearrange("p (c i j) -> p c j i", i=4, j=PACK)[:, :, 2 * u : 2 * u + 2, :]
            src = raw[0][:, 2 * u : 2 * u + 2, h * HALF + c0 : h * HALF + c1].rearrange("p j (c i) -> p c j i", i=4)
            engine_copy(dst, src)

        def vector_group(dst, src):
            nc.vector.tensor_copy(out=dst, in_=src)

        def scalar_group(dst, src):
            nc.scalar.activation(dst, src, COPY)

        def quantise(a, h):
            cols = slice(h * HALF, (h + 1) * HALF)
            nc.vector.quantize_mx(out=tok_words[a][:, cols].bitcast(FP8X4), scales=tok_scales[a][:, cols], in_=grouped[a][h][:])

        def gather_words(a, s0, s1):
            nc.vector.tensor_copy(slot_words[a][:, s0:s1], tok_words[a][:].bitcast(U32).indirect(offsets[:, s0 // 16 : s1 // 16]))

        def gather_scales(a, s0, s1):
            nc.vector.tensor_copy(slot_scales[a][:, s0:s1], tok_scales[a][:].indirect(offsets[:, s0 // 16 : s1 // 16]))

        banks = {}

        def multiply(a, t, e):
            if a == 0:
                banks[t, e] = psum.tile([P, C], F32, name="bank")
            ea = e * PASSES + a
            nc.tensor.matmul_mx(
                out=banks[t, e][:],
                lhsT=words[:, ea, 2 * P * t : 2 * P * (t + 1)].bitcast(FP4X4),
                lhsT_scale=scales[:, ea, P * t : P * (t + 1)],
                rhs=slot_words[a][:, e * C : (e + 1) * C].bitcast(FP8X4),
                rhs_scale=slot_scales[a][:, e * C : (e + 1) * C],
                start=(a == 0),
                stop=(a == PASSES - 1),
            )

        def leave_bank(t, e):
            nc.scalar.activation(y[t][:, e * C : (e + 1) * C], banks[t, e][:], IDENTITY, bias=bias[:, t, e : e + 1])

        def scatter(t, s0, s1):
            nc.vector.tensor_tensor(result[t][:].indirect(offsets[:, s0 // 16 : s1 // 16]), y[t][:, s0:s1], gates[t][:, s0:s1], MULT)

        def store(t):
            nc.sync.dma_start(out=out[t * P : (t + 1) * P, :], in_=result[t][:, :T])

        S = E * C
        for u in range(2):
            for h in range(2):
                group_pair(vector_group, h, u, 0, VCOLS)
                group_pair(scalar_group, h, u, VCOLS, HALF)
        for h in range(2):
            quantise(0, h)
        group(scalar_group, 1, 0, 0, HALF)
        group(scalar_group, 1, 1, V1, HALF)
        gather_words(0, 0, S)
        group(vector_group, 1, 1, 0, V1)
        quantise(1, 0)
        gather_scales(0, 0, HALF)
        quantise(1, 1)
        gather_scales(0, HALF, S)
        group(scalar_group, 2, 0, 0, HALF)
        group(scalar_group, 2, 1, 0, HALF)
        gather_words(1, 0, S)
        quantise(2, 0)
        gather_scales(1, 0, HALF)
        quantise(2, 1)
        gather_scales(1, HALF, S)
        for h in range(2):
            gather_words(2, h * HALF, (h + 1) * HALF)
            gather_scales(2, h * HALF, (h + 1) * HALF)
        for t in range(2):
            for e in range(2):
                for a in range(PASSES):
                    multiply(a, t, e)
                leave_bank(t, e)
            scatter(t, 0, HALF)
        for t in range(2):
            for e in range(2, E):
                for a in range(PASSES):
                    multiply(a, t, e)
                leave_bank(t, e)
            scatter(t, HALF, S)
            store(t)
        for e in range(E):
            for a in range(PASSES):
                multiply(a, 2, e)
            leave_bank(2, e)
        scatter(2, 0, S)
        store(2)
